import numpy as np
import ml_dtypes


def mxq(x, axis, fmt="e4m3"):
    dtype, down = {"e4m3": (ml_dtypes.float8_e4m3fn, 7), "e5m2": (ml_dtypes.float8_e5m2, 14)}[fmt]
    v = np.moveaxis(np.asarray(x, np.float32).astype(ml_dtypes.bfloat16).astype(np.float64), axis, -1)
    blocks = v.reshape(v.shape[:-1] + (-1, 32))
    amax = np.abs(blocks).max(-1, keepdims=True)
    byte = np.maximum(np.where(amax > 0, np.frexp(amax)[1] - 1 + 127, 0) - down, 1)
    scale = np.exp2(byte - 127.0)
    codes = (blocks / scale).astype(np.float32).astype(dtype).astype(np.float64)
    return np.moveaxis((codes * scale).reshape(v.shape), -1, axis)


WIDE = False


def mx_kscale(k, group=512):
    if not WIDE:
        return np.ones(k)
    levels = np.array([18, -18])
    if group != 512:
        return np.exp2(np.random.permutation(np.resize(levels, k // group))).repeat(group)
    if k % 512:
        return np.exp2(np.random.permutation(np.resize(levels, k // 32))).repeat(32)
    a = np.empty((k // 512, 16))
    for p in range(k // 512):
        a[p, :8] = np.random.permutation(np.resize(levels, 8))
        for g in range(8):
            far = levels[np.abs(levels - a[p, g]) >= 10]
            a[p, g + 8] = far[np.random.randint(len(far))]
    return np.exp2(a.ravel()).repeat(32)


def f64(x):
    return np.asarray(x).astype(np.float64)


G, D, M, N = 4, 128, 256, 512


def setup_inputs():
    n = np.random.standard_normal
    s_d = mx_kscale(D, 0)
    return {
        "x": (n((G, D, M)) / s_d[:, None] / np.sqrt(D)).astype(np.float32),
        "c": (n((G, D, N)) * s_d[:, None] / np.sqrt(D)).astype(np.float32),
        "xn": (np.random.uniform(0.9, 1.3, (G, M, 1))).astype(np.float32),
        "cn": (np.random.uniform(0.9, 1.3, (G, 1, N))).astype(np.float32),
    }


def reference(x, c, xn, cn):
    xq = mxq(f64(x), 1, "e4m3")
    cq = mxq(f64(c), 1, "e4m3")
    z = xq.transpose(0, 2, 1) @ cq
    d2 = f64(xn) + f64(cn) - 2.0 * z
    y = np.exp(-d2)
    return y

@@ -1,0 +1,100 @@
+from contextlib import ExitStack
+
+import concourse.mybir as mybir
+
+G, D, M, N = 4, 128, 256, 512
+FLOPS = 2 * G * D * M * N
+
+F32 = mybir.dt.float32
+BF16 = mybir.dt.bfloat16
+U32 = mybir.dt.uint32
+U8 = mybir.dt.uint8
+FP8X4 = mybir.dt.float8_e4m3fn_x4
+ALU = mybir.AluOpType
+ACT = mybir.ActivationFunctionType
+
+P = 128
+PACK = 4
+ROWS = D // PACK
+HALVES = M // P
+SQ = 32
+C_SPLIT = 320
+
+
+def interleave(copy, dst, src):
+    copy(out=dst.rearrange("p (c i) j -> p c j i", i=4), in_=src.rearrange("p j (c i) -> p c j i", i=4))
+
+
+def quantize(nc, codes, scales, grouped):
+    nc.vector.quantize_mx(out=codes.bitcast(FP8X4), scales=scales, in_=grouped.rearrange("p n j -> p (n j)"))
+
+
+def tile_rows_kern_rbf_kernel(tc, x, c, xn, cn, out):
+    nc = tc.nc
+    with ExitStack() as ctx:
+        sb = ctx.enter_context(tc.tile_pool(name="sb", bufs=1))
+        ps = ctx.enter_context(tc.psum_pool(name="ps", bufs=1))
+        ctx.enter_context(tc.manual_schedule())
+
+        c_raw = sb.tile([P, PACK, N], F32, name="c_raw")
+        x_raw = sb.tile([P, PACK, M], F32, name="x_raw")
+        xn_rows = sb.tile([P, G * HALVES * SQ], F32, name="xn_rows", align_bytes=64)
+        xn_cols = sb.tile([P, G * HALVES * SQ], F32, name="xn_cols", align_bytes=64)
+        neg_xn = sb.tile([P, G * HALVES], F32, name="neg_xn")
+        cn_all = [sb.tile([P, N], F32, name="cn_all%d" % g) for g in range(G)]
+
+        nc.sync.dma_start(out=c_raw[:], in_=c.rearrange("g (p j) n -> (g p) j n", j=PACK))
+        nc.vector.memset(xn_rows[:], 0.0)
+        nc.sync.dma_start(
+            out=xn_rows[0:P:SQ, :].rearrange("q (t i) -> q t i", i=SQ),
+            in_=xn.rearrange("g (h q i) o -> q (g h) (i o)", h=HALVES, i=SQ),
+        )
+        nc.sync.dma_start(out=x_raw[:], in_=x.rearrange("g (p j) m -> (g p) j m", j=PACK))
+        for g in range(G):
+            nc.sync.dma_start(out=cn_all[g][:], in_=cn[g, 0, :].partition_broadcast(P))
+
+        nc.vector.transpose(out=xn_cols[:], in_=xn_rows[:])
+        nc.vector.tensor_scalar(
+            out=neg_xn[:], in0=xn_cols[:, 0 : G * HALVES * SQ : SQ], scalar1=-1.0, scalar2=None, op0=ALU.mult
+        )
+
+        half = N // 2
+        c_bf = [sb.tile([P, half, PACK], BF16, name="c_bf%d" % u, align_bytes=64) for u in range(2)]
+        c_codes = sb.tile([P, N], U32, name="c_codes", align_bytes=64)
+        c_scales = sb.tile([P, N], U8, name="c_scales", align_bytes=64)
+        x_bf = [sb.tile([P, P, PACK], BF16, name="x_bf%d" % h, align_bytes=64) for h in range(HALVES)]
+        x_codes = [sb.tile([P, P], U32, name="x_codes%d" % h, align_bytes=64) for h in range(HALVES)]
+        x_scales = [sb.tile([P, P], U8, name="x_scales%d" % h, align_bytes=64) for h in range(HALVES)]
+
+        interleave(nc.scalar.copy, c_bf[1][:, C_SPLIT - half :, :], c_raw[:, :, C_SPLIT:])
+        interleave(nc.vector.tensor_copy, c_bf[0][:], c_raw[:, :, :half])
+        interleave(nc.vector.tensor_copy, c_bf[1][:, : C_SPLIT - half, :], c_raw[:, :, half:C_SPLIT])
+        for u in range(2):
+            cols = slice(u * half, (u + 1) * half)
+            quantize(nc, c_codes[:, cols], c_scales[:, cols], c_bf[u][:])
+        interleave(nc.scalar.copy, x_bf[0][:], x_raw[:, :, :P])
+        interleave(nc.vector.tensor_copy, x_bf[1][:], x_raw[:, :, P:])
+        for h in range(HALVES):
+            quantize(nc, x_codes[h][:], x_scales[h][:], x_bf[h][:])
+
+        for g in range(G):
+            rows = slice(g * ROWS, (g + 1) * ROWS)
+            for h in range(HALVES):
+                t = g * HALVES + h
+                z = ps.tile([P, N], F32, name="z%d" % t)
+                nc.tensor.matmul_mx(
+                    out=z[:],
+                    lhsT=x_codes[h][rows, :].bitcast(FP8X4),
+                    lhsT_scale=x_scales[h][rows, :],
+                    rhs=c_codes[rows, :].bitcast(FP8X4),
+                    rhs_scale=c_scales[rows, :],
+                    start=True,
+                    stop=True,
+                )
+                arg = sb.tile([P, N], F32, name="arg%d" % t)
+                nc.vector.scalar_tensor_tensor(
+                    out=arg[:], in0=z[:], scalar=2.0, in1=cn_all[g][:], op0=ALU.mult, op1=ALU.subtract
+                )
+                res = sb.tile([P, N], F32, name="res%d" % t)
+                nc.scalar.activation(out=res[:], in_=arg[:], func=ACT.Exp, bias=neg_xn[:, t : t + 1], scale=1.0)
+                nc.sync.dma_start(out=out[g, h * P : (h + 1) * P, :], in_=res[:])

@@ -18,7 +18,8 @@ PACK = 4
 ROWS = D // PACK
 HALVES = M // P
 SQ = 32
-C_SPLIT = 320
+C_SPLIT = 288
+EARLY = 2
 
 
 def interleave(copy, dst, src):
@@ -41,8 +42,17 @@ def tile_rows_kern_rbf_kernel(tc, x, c, xn, cn, out):
         xn_rows = sb.tile([P, G * HALVES * SQ], F32, name="xn_rows", align_bytes=64)
         xn_cols = sb.tile([P, G * HALVES * SQ], F32, name="xn_cols", align_bytes=64)
         neg_xn = sb.tile([P, G * HALVES], F32, name="neg_xn")
-        cn_all = [sb.tile([P, N], F32, name="cn_all%d" % g) for g in range(G)]
+        cn_rows = sb.tile([P, SQ], F32, name="cn_rows", align_bytes=64)
+        cn_cols = sb.tile([P, SQ], F32, name="cn_cols", align_bytes=64)
+        cn_wide = [sb.tile([P, N], F32, name="cn_wide%d" % g, align_bytes=64) for g in range(EARLY)]
+        cn_early = [sb.tile([P, N], F32, name="cn_early%d" % g, align_bytes=64) for g in range(EARLY)]
+        cn_late = sb.tile([P, (G - EARLY) * N], F32, name="cn_late")
+        cn_flat = cn.rearrange("g o n -> (g o n)")
 
+        nc.sync.dma_start(
+            out=cn_rows[:],
+            in_=cn_flat[: EARLY * N].partition_broadcast(P // SQ).rearrange("q (b i) -> q b i", i=SQ),
+        )
         nc.sync.dma_start(out=c_raw[:], in_=c.rearrange("g (p j) n -> (g p) j n", j=PACK))
         nc.vector.memset(xn_rows[:], 0.0)
         nc.sync.dma_start(
@@ -50,13 +60,18 @@ def tile_rows_kern_rbf_kernel(tc, x, c, xn, cn, out):
             in_=xn.rearrange("g (h q i) o -> q (g h) (i o)", h=HALVES, i=SQ),
         )
         nc.sync.dma_start(out=x_raw[:], in_=x.rearrange("g (p j) m -> (g p) j m", j=PACK))
-        for g in range(G):
-            nc.sync.dma_start(out=cn_all[g][:], in_=cn[g, 0, :].partition_broadcast(P))
+        nc.sync.dma_start(out=cn_late[:], in_=cn_flat[EARLY * N :].partition_broadcast(P))
 
-        nc.vector.transpose(out=xn_cols[:], in_=xn_rows[:])
-        nc.vector.tensor_scalar(
-            out=neg_xn[:], in0=xn_cols[:, 0 : G * HALVES * SQ : SQ], scalar1=-1.0, scalar2=None, op0=ALU.mult
-        )
+        nc.vector.transpose(out=cn_cols[:], in_=cn_rows[:])
+        blocks = N // SQ
+        for g in range(EARLY):
+            nc.scalar.copy(
+                out=cn_wide[g][:].rearrange("p (b j) -> p b j", j=SQ),
+                in_=cn_cols[:, g * blocks : (g + 1) * blocks].unsqueeze(2).to_broadcast([P, blocks, SQ]),
+            )
+        for g in range(EARLY):
+            nc.vector.transpose(out=cn_early[g][:], in_=cn_wide[g][:])
+        cn_all = [tile[:] for tile in cn_early] + [cn_late[:, u * N : (u + 1) * N] for u in range(G - EARLY)]
 
         half = N // 2
         c_bf = [sb.tile([P, half, PACK], BF16, name="c_bf%d" % u, align_bytes=64) for u in range(2)]
@@ -73,9 +88,13 @@ def tile_rows_kern_rbf_kernel(tc, x, c, xn, cn, out):
             cols = slice(u * half, (u + 1) * half)
             quantize(nc, c_codes[:, cols], c_scales[:, cols], c_bf[u][:])
         interleave(nc.scalar.copy, x_bf[0][:], x_raw[:, :, :P])
-        interleave(nc.vector.tensor_copy, x_bf[1][:], x_raw[:, :, P:])
-        for h in range(HALVES):
-            quantize(nc, x_codes[h][:], x_scales[h][:], x_bf[h][:])
+        interleave(nc.scalar.copy, x_bf[1][:], x_raw[:, :, P:])
+        quantize(nc, x_codes[0][:], x_scales[0][:], x_bf[0][:])
+        nc.vector.transpose(out=xn_cols[:], in_=xn_rows[:])
+        quantize(nc, x_codes[1][:], x_scales[1][:], x_bf[1][:])
+        nc.vector.tensor_scalar(
+            out=neg_xn[:], in0=xn_cols[:, 0 : G * HALVES * SQ : SQ], scalar1=-1.0, scalar2=None, op0=ALU.mult
+        )
 
         for g in range(G):
             rows = slice(g * ROWS, (g + 1) * ROWS)
@@ -93,7 +112,7 @@ def tile_rows_kern_rbf_kernel(tc, x, c, xn, cn, out):
                 )
                 arg = sb.tile([P, N], F32, name="arg%d" % t)
                 nc.vector.scalar_tensor_tensor(
-                    out=arg[:], in0=z[:], scalar=2.0, in1=cn_all[g][:], op0=ALU.mult, op1=ALU.subtract
+                    out=arg[:], in0=z[:], scalar=2.0, in1=cn_all[g], op0=ALU.mult, op1=ALU.subtract
                 )
                 res = sb.tile([P, N], F32, name="res%d" % t)
                 nc.scalar.activation(out=res[:], in_=arg[:], func=ACT.Exp, bias=neg_xn[:, t : t + 1], scale=1.0)

@@ -18,8 +18,10 @@ PACK = 4
 ROWS = D // PACK
 HALVES = M // P
 SQ = 32
-C_SPLIT = 288
+C_SPLIT = 96
+A_SPLIT = 64
 EARLY = 2
+X_SPLIT = 48
 
 
 def interleave(copy, dst, src):
@@ -37,7 +39,8 @@ def tile_rows_kern_rbf_kernel(tc, x, c, xn, cn, out):
         ps = ctx.enter_context(tc.psum_pool(name="ps", bufs=1))
         ctx.enter_context(tc.manual_schedule())
 
-        c_raw = sb.tile([P, PACK, N], F32, name="c_raw")
+        half = N // 2
+        c_raw = [sb.tile([P, PACK, half], F32, name="c_raw%d" % u) for u in range(2)]
         x_raw = sb.tile([P, PACK, M], F32, name="x_raw")
         xn_rows = sb.tile([P, G * HALVES * SQ], F32, name="xn_rows", align_bytes=64)
         xn_cols = sb.tile([P, G * HALVES * SQ], F32, name="xn_cols", align_bytes=64)
@@ -53,67 +56,111 @@ def tile_rows_kern_rbf_kernel(tc, x, c, xn, cn, out):
             out=cn_rows[:],
             in_=cn_flat[: EARLY * N].partition_broadcast(P // SQ).rearrange("q (b i) -> q b i", i=SQ),
         )
-        nc.sync.dma_start(out=c_raw[:], in_=c.rearrange("g (p j) n -> (g p) j n", j=PACK))
+        c_view = c.rearrange("g (p j) n -> (g p) j n", j=PACK)
+        nc.sync.dma_start(out=c_raw[0][:], in_=c_view[:, :, :half])
+        nc.sync.dma_start(out=x_raw[:], in_=x.rearrange("g (p j) m -> (g p) j m", j=PACK))
         nc.vector.memset(xn_rows[:], 0.0)
         nc.sync.dma_start(
             out=xn_rows[0:P:SQ, :].rearrange("q (t i) -> q t i", i=SQ),
             in_=xn.rearrange("g (h q i) o -> q (g h) (i o)", h=HALVES, i=SQ),
         )
-        nc.sync.dma_start(out=x_raw[:], in_=x.rearrange("g (p j) m -> (g p) j m", j=PACK))
+        nc.sync.dma_start(out=c_raw[1][:], in_=c_view[:, :, half:])
         nc.sync.dma_start(out=cn_late[:], in_=cn_flat[EARLY * N :].partition_broadcast(P))
 
         nc.vector.transpose(out=cn_cols[:], in_=cn_rows[:])
         blocks = N // SQ
-        for g in range(EARLY):
-            nc.scalar.copy(
-                out=cn_wide[g][:].rearrange("p (b j) -> p b j", j=SQ),
-                in_=cn_cols[:, g * blocks : (g + 1) * blocks].unsqueeze(2).to_broadcast([P, blocks, SQ]),
+        shares = (
+            (nc.vector.tensor_copy, 0, 0, blocks // 2),
+            (nc.scalar.copy, 0, blocks // 2, blocks),
+            (nc.scalar.copy, 1, 0, blocks),
+        )
+        for copy, g, b0, b1 in shares:
+            copy(
+                out=cn_wide[g][:, b0 * SQ : b1 * SQ].rearrange("p (b j) -> p b j", j=SQ),
+                in_=cn_cols[:, g * blocks + b0 : g * blocks + b1].unsqueeze(2).to_broadcast([P, b1 - b0, SQ]),
             )
         for g in range(EARLY):
             nc.vector.transpose(out=cn_early[g][:], in_=cn_wide[g][:])
         cn_all = [tile[:] for tile in cn_early] + [cn_late[:, u * N : (u + 1) * N] for u in range(G - EARLY)]
 
-        half = N // 2
         c_bf = [sb.tile([P, half, PACK], BF16, name="c_bf%d" % u, align_bytes=64) for u in range(2)]
-        c_codes = sb.tile([P, N], U32, name="c_codes", align_bytes=64)
-        c_scales = sb.tile([P, N], U8, name="c_scales", align_bytes=64)
+        c_codes = [sb.tile([P, half], U32, name="c_codes%d" % u, align_bytes=64) for u in range(2)]
+        c_scales = [sb.tile([P, half], U8, name="c_scales%d" % u, align_bytes=64) for u in range(2)]
         x_bf = [sb.tile([P, P, PACK], BF16, name="x_bf%d" % h, align_bytes=64) for h in range(HALVES)]
         x_codes = [sb.tile([P, P], U32, name="x_codes%d" % h, align_bytes=64) for h in range(HALVES)]
         x_scales = [sb.tile([P, P], U8, name="x_scales%d" % h, align_bytes=64) for h in range(HALVES)]
 
-        interleave(nc.scalar.copy, c_bf[1][:, C_SPLIT - half :, :], c_raw[:, :, C_SPLIT:])
-        interleave(nc.vector.tensor_copy, c_bf[0][:], c_raw[:, :, :half])
-        interleave(nc.vector.tensor_copy, c_bf[1][:, : C_SPLIT - half, :], c_raw[:, :, half:C_SPLIT])
-        for u in range(2):
-            cols = slice(u * half, (u + 1) * half)
-            quantize(nc, c_codes[:, cols], c_scales[:, cols], c_bf[u][:])
-        interleave(nc.scalar.copy, x_bf[0][:], x_raw[:, :, :P])
+        z = [ps.tile([P, N], F32, name="z%d" % t) for t in range(G * HALVES)]
+        arg = [sb.tile([P, N], F32, name="arg%d" % t) for t in range(G * HALVES)]
+        res = [sb.tile([P, N], F32, name="res%d" % t) for t in range(G * HALVES)]
+
+        def multiply(g, h, u):
+            rows = slice(g * ROWS, (g + 1) * ROWS)
+            for n0 in range(0, half, P):
+                nc.tensor.matmul_mx(
+                    out=z[g * HALVES + h][:, u * half + n0 : u * half + n0 + P],
+                    lhsT=x_codes[h][rows, :].bitcast(FP8X4),
+                    lhsT_scale=x_scales[h][rows, :],
+                    rhs=c_codes[u][rows, n0 : n0 + P].bitcast(FP8X4),
+                    rhs_scale=c_scales[u][rows, n0 : n0 + P],
+                    start=True,
+                    stop=True,
+                )
+
+        def finish(g, h, cols):
+            t = g * HALVES + h
+            nc.vector.scalar_tensor_tensor(
+                out=arg[t][:, cols],
+                in0=z[t][:, cols],
+                scalar=2.0,
+                in1=cn_all[g][:, cols],
+                op0=ALU.mult,
+                op1=ALU.subtract,
+            )
+            nc.scalar.activation(
+                out=res[t][:, cols], in_=arg[t][:, cols], func=ACT.Exp, bias=neg_xn[:, t : t + 1], scale=1.0
+            )
+
+        def store(g, h, cols):
+            nc.sync.dma_start(out=out[g, h * P : (h + 1) * P, cols], in_=res[g * HALVES + h][:, cols])
+
+        early = [(g, h) for h in range(HALVES) for g in range(EARLY)]
+        late = [(g, h) for h in range(HALVES) for g in range(EARLY, G)]
+
+        interleave(nc.scalar.copy, c_bf[0][:, A_SPLIT:, :], c_raw[0][:, :, A_SPLIT:])
+        interleave(nc.vector.tensor_copy, c_bf[0][:, :A_SPLIT, :], c_raw[0][:, :, :A_SPLIT])
+        interleave(nc.scalar.copy, x_bf[0][:, X_SPLIT:, :], x_raw[:, :, X_SPLIT:P])
+        interleave(nc.vector.tensor_copy, x_bf[0][:, :X_SPLIT, :], x_raw[:, :, :X_SPLIT])
+        quantize(nc, c_codes[0][:], c_scales[0][:], c_bf[0][:])
         interleave(nc.scalar.copy, x_bf[1][:], x_raw[:, :, P:])
         quantize(nc, x_codes[0][:], x_scales[0][:], x_bf[0][:])
         nc.vector.transpose(out=xn_cols[:], in_=xn_rows[:])
         quantize(nc, x_codes[1][:], x_scales[1][:], x_bf[1][:])
-        nc.vector.tensor_scalar(
-            out=neg_xn[:], in0=xn_cols[:, 0 : G * HALVES * SQ : SQ], scalar1=-1.0, scalar2=None, op0=ALU.mult
-        )
+        nc.scalar.mul(out=neg_xn[:], in_=xn_cols[:, 0 : G * HALVES * SQ : SQ], mul=-1.0)
+        interleave(nc.scalar.copy, c_bf[1][:, C_SPLIT:, :], c_raw[1][:, :, C_SPLIT:])
 
-        for g in range(G):
-            rows = slice(g * ROWS, (g + 1) * ROWS)
-            for h in range(HALVES):
-                t = g * HALVES + h
-                z = ps.tile([P, N], F32, name="z%d" % t)
-                nc.tensor.matmul_mx(
-                    out=z[:],
-                    lhsT=x_codes[h][rows, :].bitcast(FP8X4),
-                    lhsT_scale=x_scales[h][rows, :],
-                    rhs=c_codes[rows, :].bitcast(FP8X4),
-                    rhs_scale=c_scales[rows, :],
-                    start=True,
-                    stop=True,
-                )
-                arg = sb.tile([P, N], F32, name="arg%d" % t)
-                nc.vector.scalar_tensor_tensor(
-                    out=arg[:], in0=z[:], scalar=2.0, in1=cn_all[g], op0=ALU.mult, op1=ALU.subtract
-                )
-                res = sb.tile([P, N], F32, name="res%d" % t)
-                nc.scalar.activation(out=res[:], in_=arg[:], func=ACT.Exp, bias=neg_xn[:, t : t + 1], scale=1.0)
-                nc.sync.dma_start(out=out[g, h * P : (h + 1) * P, :], in_=res[:])
+
+        left, right = slice(0, half), slice(half, N)
+        for g, h in early + late[: G - EARLY]:
+            multiply(g, h, 0)
+        for step, (g, h) in enumerate(early):
+            finish(g, h, left)
+            store(g, h, left)
+            if step == 0:
+                interleave(nc.vector.tensor_copy, c_bf[1][:, :C_SPLIT, :], c_raw[1][:, :, :C_SPLIT])
+            if step == 1:
+                quantize(nc, c_codes[1][:], c_scales[1][:], c_bf[1][:])
+        for g, h in early:
+            multiply(g, h, 1)
+            finish(g, h, right)
+            store(g, h, right)
+        for g, h in late:
+            if h > 0:
+                multiply(g, h, 0)
+            multiply(g, h, 1)
+            for cols in (left, right):
+                finish(g, h, cols)
+                if (g, h) == late[-1]:
+                    store(g, h, cols)
+            if (g, h) != late[-1]:
+                store(g, h, slice(0, N))

from contextlib import ExitStack

import concourse.mybir as mybir

G, D, M, N = 4, 128, 256, 512
FLOPS = 2 * G * D * M * N

F32 = mybir.dt.float32
BF16 = mybir.dt.bfloat16
U32 = mybir.dt.uint32
U8 = mybir.dt.uint8
FP8X4 = mybir.dt.float8_e4m3fn_x4
ALU = mybir.AluOpType
ACT = mybir.ActivationFunctionType

P = 128
PACK = 4
ROWS = D // PACK
HALVES = M // P
SQ = 32
C_SPLIT = 96
A_SPLIT = 64
EARLY = 2
X_SPLIT = 48


def interleave(copy, dst, src):
    copy(out=dst.rearrange("p (c i) j -> p c j i", i=4), in_=src.rearrange("p j (c i) -> p c j i", i=4))


def quantize(nc, codes, scales, grouped):
    nc.vector.quantize_mx(out=codes.bitcast(FP8X4), scales=scales, in_=grouped.rearrange("p n j -> p (n j)"))


def tile_rows_kern_rbf_kernel(tc, x, c, xn, cn, out):
    nc = tc.nc
    with ExitStack() as ctx:
        sb = ctx.enter_context(tc.tile_pool(name="sb", bufs=1))
        ps = ctx.enter_context(tc.psum_pool(name="ps", bufs=1))
        ctx.enter_context(tc.manual_schedule())

        half = N // 2
        c_raw = [sb.tile([P, PACK, half], F32, name="c_raw%d" % u) for u in range(2)]
        x_raw = sb.tile([P, PACK, M], F32, name="x_raw")
        xn_rows = sb.tile([P, G * HALVES * SQ], F32, name="xn_rows", align_bytes=64)
        xn_cols = sb.tile([P, G * HALVES * SQ], F32, name="xn_cols", align_bytes=64)
        neg_xn = sb.tile([P, G * HALVES], F32, name="neg_xn")
        cn_rows = sb.tile([P, SQ], F32, name="cn_rows", align_bytes=64)
        cn_cols = sb.tile([P, SQ], F32, name="cn_cols", align_bytes=64)
        cn_wide = [sb.tile([P, N], F32, name="cn_wide%d" % g, align_bytes=64) for g in range(EARLY)]
        cn_early = [sb.tile([P, N], F32, name="cn_early%d" % g, align_bytes=64) for g in range(EARLY)]
        cn_late = sb.tile([P, (G - EARLY) * N], F32, name="cn_late")
        cn_flat = cn.rearrange("g o n -> (g o n)")

        nc.sync.dma_start(
            out=cn_rows[:],
            in_=cn_flat[: EARLY * N].partition_broadcast(P // SQ).rearrange("q (b i) -> q b i", i=SQ),
        )
        c_view = c.rearrange("g (p j) n -> (g p) j n", j=PACK)
        nc.sync.dma_start(out=c_raw[0][:], in_=c_view[:, :, :half])
        nc.sync.dma_start(out=x_raw[:], in_=x.rearrange("g (p j) m -> (g p) j m", j=PACK))
        nc.vector.memset(xn_rows[:], 0.0)
        nc.sync.dma_start(
            out=xn_rows[0:P:SQ, :].rearrange("q (t i) -> q t i", i=SQ),
            in_=xn.rearrange("g (h q i) o -> q (g h) (i o)", h=HALVES, i=SQ),
        )
        nc.sync.dma_start(out=c_raw[1][:], in_=c_view[:, :, half:])
        nc.sync.dma_start(out=cn_late[:], in_=cn_flat[EARLY * N :].partition_broadcast(P))

        nc.vector.transpose(out=cn_cols[:], in_=cn_rows[:])
        blocks = N // SQ
        shares = (
            (nc.vector.tensor_copy, 0, 0, blocks // 2),
            (nc.scalar.copy, 0, blocks // 2, blocks),
            (nc.scalar.copy, 1, 0, blocks),
        )
        for copy, g, b0, b1 in shares:
            copy(
                out=cn_wide[g][:, b0 * SQ : b1 * SQ].rearrange("p (b j) -> p b j", j=SQ),
                in_=cn_cols[:, g * blocks + b0 : g * blocks + b1].unsqueeze(2).to_broadcast([P, b1 - b0, SQ]),
            )
        for g in range(EARLY):
            nc.vector.transpose(out=cn_early[g][:], in_=cn_wide[g][:])
        cn_all = [tile[:] for tile in cn_early] + [cn_late[:, u * N : (u + 1) * N] for u in range(G - EARLY)]

        c_bf = [sb.tile([P, half, PACK], BF16, name="c_bf%d" % u, align_bytes=64) for u in range(2)]
        c_codes = [sb.tile([P, half], U32, name="c_codes%d" % u, align_bytes=64) for u in range(2)]
        c_scales = [sb.tile([P, half], U8, name="c_scales%d" % u, align_bytes=64) for u in range(2)]
        x_bf = [sb.tile([P, P, PACK], BF16, name="x_bf%d" % h, align_bytes=64) for h in range(HALVES)]
        x_codes = [sb.tile([P, P], U32, name="x_codes%d" % h, align_bytes=64) for h in range(HALVES)]
        x_scales = [sb.tile([P, P], U8, name="x_scales%d" % h, align_bytes=64) for h in range(HALVES)]

        z = [ps.tile([P, N], F32, name="z%d" % t) for t in range(G * HALVES)]
        arg = [sb.tile([P, N], F32, name="arg%d" % t) for t in range(G * HALVES)]
        res = [sb.tile([P, N], F32, name="res%d" % t) for t in range(G * HALVES)]

        def multiply(g, h, u):
            rows = slice(g * ROWS, (g + 1) * ROWS)
            for n0 in range(0, half, P):
                nc.tensor.matmul_mx(
                    out=z[g * HALVES + h][:, u * half + n0 : u * half + n0 + P],
                    lhsT=x_codes[h][rows, :].bitcast(FP8X4),
                    lhsT_scale=x_scales[h][rows, :],
                    rhs=c_codes[u][rows, n0 : n0 + P].bitcast(FP8X4),
                    rhs_scale=c_scales[u][rows, n0 : n0 + P],
                    start=True,
                    stop=True,
                )

        def finish(g, h, cols):
            t = g * HALVES + h
            nc.vector.scalar_tensor_tensor(
                out=arg[t][:, cols],
                in0=z[t][:, cols],
                scalar=2.0,
                in1=cn_all[g][:, cols],
                op0=ALU.mult,
                op1=ALU.subtract,
            )
            nc.scalar.activation(
                out=res[t][:, cols], in_=arg[t][:, cols], func=ACT.Exp, bias=neg_xn[:, t : t + 1], scale=1.0
            )

        def store(g, h, cols):
            nc.sync.dma_start(out=out[g, h * P : (h + 1) * P, cols], in_=res[g * HALVES + h][:, cols])

        early = [(g, h) for h in range(HALVES) for g in range(EARLY)]
        late = [(g, h) for h in range(HALVES) for g in range(EARLY, G)]

        interleave(nc.scalar.copy, c_bf[0][:, A_SPLIT:, :], c_raw[0][:, :, A_SPLIT:])
        interleave(nc.vector.tensor_copy, c_bf[0][:, :A_SPLIT, :], c_raw[0][:, :, :A_SPLIT])
        interleave(nc.scalar.copy, x_bf[0][:, X_SPLIT:, :], x_raw[:, :, X_SPLIT:P])
        interleave(nc.vector.tensor_copy, x_bf[0][:, :X_SPLIT, :], x_raw[:, :, :X_SPLIT])
        quantize(nc, c_codes[0][:], c_scales[0][:], c_bf[0][:])
        interleave(nc.scalar.copy, x_bf[1][:], x_raw[:, :, P:])
        quantize(nc, x_codes[0][:], x_scales[0][:], x_bf[0][:])
        nc.vector.transpose(out=xn_cols[:], in_=xn_rows[:])
        quantize(nc, x_codes[1][:], x_scales[1][:], x_bf[1][:])
        nc.scalar.mul(out=neg_xn[:], in_=xn_cols[:, 0 : G * HALVES * SQ : SQ], mul=-1.0)
        interleave(nc.scalar.copy, c_bf[1][:, C_SPLIT:, :], c_raw[1][:, :, C_SPLIT:])


        left, right = slice(0, half), slice(half, N)
        for g, h in early + late[: G - EARLY]:
            multiply(g, h, 0)
        for step, (g, h) in enumerate(early):
            finish(g, h, left)
            store(g, h, left)
            if step == 0:
                interleave(nc.vector.tensor_copy, c_bf[1][:, :C_SPLIT, :], c_raw[1][:, :, :C_SPLIT])
            if step == 1:
                quantize(nc, c_codes[1][:], c_scales[1][:], c_bf[1][:])
        for g, h in early:
            multiply(g, h, 1)
            finish(g, h, right)
            store(g, h, right)
        for g, h in late:
            if h > 0:
                multiply(g, h, 0)
            multiply(g, h, 1)
            for cols in (left, right):
                finish(g, h, cols)
                if (g, h) == late[-1]:
                    store(g, h, cols)
            if (g, h) != late[-1]:
                store(g, h, slice(0, N))
